import numpy as np
import ml_dtypes


def mxq(x, axis, fmt="e4m3"):
    dtype, down = {"e4m3": (ml_dtypes.float8_e4m3fn, 7), "e5m2": (ml_dtypes.float8_e5m2, 14)}[fmt]
    v = np.moveaxis(np.asarray(x, np.float32).astype(ml_dtypes.bfloat16).astype(np.float64), axis, -1)
    blocks = v.reshape(v.shape[:-1] + (-1, 32))
    amax = np.abs(blocks).max(-1, keepdims=True)
    byte = np.maximum(np.where(amax > 0, np.frexp(amax)[1] - 1 + 127, 0) - down, 1)
    scale = np.exp2(byte - 127.0)
    codes = (blocks / scale).astype(np.float32).astype(dtype).astype(np.float64)
    return np.moveaxis((codes * scale).reshape(v.shape), -1, axis)


WIDE = False


def mx_kscale(k):
    if not WIDE:
        return np.ones(k)
    levels = np.array([10, -10, 5, -5, 0])
    if k % 512:
        return np.exp2(np.random.permutation(np.resize(levels, k // 32))).repeat(32)
    a = np.empty((k // 512, 16))
    for p in range(k // 512):
        a[p, :8] = np.random.permutation(np.resize(levels, 8))
        for g in range(8):
            far = levels[np.abs(levels - a[p, g]) >= 10]
            a[p, g + 8] = far[np.random.randint(len(far))]
    return np.exp2(a.ravel()).repeat(32)


def f64(x):
    return np.asarray(x).astype(np.float64)


def striped(idx):
    return np.tile(np.asarray(idx).reshape(-1, 16).T, (8, 1)).astype(np.uint16)


def unstriped(offs):
    return offs[:16].T.reshape(-1).astype(np.int64)


E2M1 = np.array([0.0, 0.5, 1.0, 1.5, 2.0, 3.0, 4.0, 6.0, -0.0, -0.5, -1.0, -1.5, -2.0, -3.0, -4.0, -6.0])


def pack_weight(w, fmt):
    k, n = w.shape
    w = f64(np.asarray(w, np.float32).astype(ml_dtypes.bfloat16)).reshape(k // 32, 32, n)
    amax = np.abs(w).max(1)
    if fmt == "e4m3":
        byte = np.frexp(amax)[1] - 1 + 127 - 7
    else:
        mant, ex = np.frexp(amax / 6.0)
        byte = np.where(mant > 0.5, ex, ex - 1) + 127
    byte = np.clip(np.where(amax > 0, byte, 1), 1, 254)
    scaled = (w * np.exp2(127.0 - byte)[:, None, :]).reshape(k, n).astype(np.float32)
    by_word = np.ascontiguousarray(scaled.reshape(k // 512, 128, 4, n).transpose(0, 1, 3, 2))
    if fmt == "e4m3":
        words = by_word.astype(ml_dtypes.float8_e4m3fn).view(np.uint8)
    else:
        c = by_word.astype(ml_dtypes.float4_e2m1fn).view(np.uint8) & 0xF
        words = (c[..., 0::2] | (c[..., 1::2] << 4)).reshape(k // 512, 128, 2 * n)
    return np.ascontiguousarray(words), np.ascontiguousarray(byte.astype(np.uint8).reshape(k // 512, 16, n))


def unpack_weight(words, scales, fmt):
    g, _, n = scales.shape
    words = np.ascontiguousarray(words).reshape(g, 128, n, -1)
    if fmt == "e4m3":
        vals = words.view(ml_dtypes.float8_e4m3fn).astype(np.float64)
    else:
        nib = np.empty((g, 128, n, 4), np.uint8)
        nib[..., 0::2] = words & 0xF
        nib[..., 1::2] = words >> 4
        vals = E2M1[nib]
    vals = vals * np.repeat(np.exp2(scales.astype(np.float64) - 127.0), 8, axis=1)[..., None]
    return vals.transpose(0, 1, 3, 2).reshape(g * 512, n)


D, T, I, U, J, Q, E = 512, 2048, 512, 1024, 256, 256, 512


def setup_inputs():
    n = np.random.standard_normal
    idx = np.random.permutation(T)[:I]
    idx2 = np.random.permutation(U)[:J]
    fd = mx_kscale(D)
    fi = mx_kscale(I)
    ti = np.ones(T)
    ti[idx] = fi
    keysp = pack_weight(n((D, T)) / fd[:, None], "e2m1")
    return {
        "query": (n((D, Q)) * 0.4 / np.sqrt(D) * fd[:, None]).astype(np.float32),
        "keys_words": keysp[0],
        "keys_scales": keysp[1],
        "size": (np.random.uniform(0.5, 2.0, (1, I)) * fi).astype(np.float32),
        "vals": (n((E, T)) / ti).astype(np.float32),
        "back": (0.3 * n((E, 1)) + 0.5 * n((E, U))).astype(np.float32),
        "ff": (np.random.uniform(0.2, 1.0, (E, 1))).astype(np.float32),
        "offs": striped(idx),
        "offs2": striped(idx2),
    }


def reference(query, keys_words, keys_scales, size, vals, back, ff, offs, offs2):
    idx = unstriped(offs)
    idx2 = unstriped(offs2)
    keysu = unpack_weight(keys_words, keys_scales, "e2m1")
    queryq = mxq(f64(query), 0, "e4m3")
    keysidxg = keysu[:, idx]
    a = queryq.T @ keysidxg
    p = np.exp(a - np.max(a, axis=1, keepdims=True))
    w = p * f64(size) / np.sum(p, axis=1, keepdims=True)
    wt = w.T
    vt = f64(vals)[:, idx].T
    vtq = mxq(vt, 0, "e4m3")
    wtq = mxq(wt, 0, "e4m3")
    o = vtq.T @ wtq
    mb = np.mean(f64(back)[:, idx2], axis=1, keepdims=True) * f64(ff)
    y = o - mb
    return y

@@ -1,0 +1,146 @@
+from contextlib import ExitStack
+
+import concourse.mybir as mybir
+from concourse.masks import make_identity
+
+D, T, I, U, J, Q, E = 512, 2048, 512, 1024, 256, 256, 512
+FLOPS = 2 * Q * I * D + 2 * E * Q * I
+
+F32 = mybir.dt.float32
+BF16 = mybir.dt.bfloat16
+I32 = mybir.dt.int32
+U32 = mybir.dt.uint32
+U16 = mybir.dt.uint16
+U8 = mybir.dt.uint8
+FP8X4 = mybir.dt.float8_e4m3fn_x4
+FP4X4 = mybir.dt.float4_e2m1fn_x4
+ALU = mybir.AluOpType
+ACT = mybir.ActivationFunctionType
+AXIS = mybir.AxisListType
+
+P = 128
+PACK = 4
+HALVES = Q // P
+TILES = E // P
+
+
+def tile_attend_relativeread_kernel(tc, query, keys_words, keys_scales, size, vals, back, ff, offs, offs2, out):
+    nc = tc.nc
+    with ExitStack() as ctx:
+        sb = ctx.enter_context(tc.tile_pool(name="sb", bufs=1))
+        ps = ctx.enter_context(tc.psum_pool(name="ps", bufs=1))
+        ps_turn = ctx.enter_context(tc.psum_pool(name="ps_turn", bufs=2))
+
+        slots = sb.tile([P, I // 16], U16)
+        slots2 = sb.tile([P, J // 16], U16)
+        key_words = sb.tile([P, T], U16, align_bytes=64)
+        key_bytes = sb.tile([P, T], U8, align_bytes=64)
+        q_raw = sb.tile([P, PACK, Q], F32)
+        size_cols = sb.tile([P, PACK], F32)
+        ff_cols = sb.tile([P, TILES], F32)
+        val_pool = [sb.tile([P, T], F32, name="val_pool%d" % j) for j in range(TILES)]
+        back_pool = [sb.tile([P, U], F32, name="back_pool%d" % j) for j in range(TILES)]
+        ident = sb.tile([P, P], F32)
+
+        nc.gpsimd.memset(key_bytes[:].bitcast(I32), 0)
+        vals_by_tile = vals.rearrange("(p j) t -> j p t", j=TILES)
+        back_by_tile = back.rearrange("(p j) u -> j p u", j=TILES)
+        nc.gpsimd.dma_start(size_cols[:], size.rearrange("o (p t) -> p (o t)", t=PACK))
+        nc.sync.dma_start(key_words[:].bitcast(I32), keys_words[0].bitcast(I32))
+        nc.sync.dma_start(slots[:], offs)
+        nc.sync.dma_start(q_raw[:], query.rearrange("(p t) q -> p t q", t=PACK))
+        for r in range(4):
+            nc.sync.dma_start(
+                key_bytes[32 * r : 32 * r + 4, :].bitcast(I32), keys_scales[0, 4 * r : 4 * r + 4, :].bitcast(I32)
+            )
+        for j in range(TILES - 1):
+            nc.sync.dma_start(val_pool[j][:], vals_by_tile[j])
+        nc.sync.dma_start(slots2[:], offs2)
+        nc.sync.dma_start(ff_cols[:], ff.rearrange("(p j) o -> p (j o)", j=TILES))
+        nc.sync.dma_start(val_pool[TILES - 1][:], vals_by_tile[TILES - 1])
+        for j in range(TILES):
+            nc.sync.dma_start(back_pool[j][:], back_by_tile[j])
+        make_identity(nc, ident[:])
+
+        k_words = sb.tile([P, I], U16, align_bytes=64)
+        k_bytes = sb.tile([P, I], U8, align_bytes=64)
+        nc.vector.tensor_copy(k_words[:], key_words[:].indirect(slots[:]))
+        nc.vector.tensor_copy(k_bytes[:], key_bytes[:].indirect(slots[:]))
+
+        q_bf = sb.tile([P, Q, PACK], BF16, align_bytes=64)
+        q_codes = sb.tile([P, Q], U32, align_bytes=64)
+        q_scales = sb.tile([P, Q], U8, align_bytes=64)
+        nc.scalar.copy(q_bf[:], q_raw[:].rearrange("p t q -> p q t"))
+        nc.vector.quantize_mx(q_codes[:].bitcast(FP8X4), q_scales[:], q_bf[:].rearrange("p q t -> p (q t)"))
+
+        size_rows = ps.tile([P, PACK, P], F32)
+        for t in range(PACK):
+            nc.tensor.transpose(size_rows[:, t, :], size_cols[:, t : t + 1].to_broadcast([P, P]), ident[:])
+
+        w_turned = ps.tile([P, HALVES, 2, P], F32)
+        for h in range(HALVES):
+            cols = slice(h * P, (h + 1) * P)
+            scores = ps.tile([P, I], F32, name="scores%d" % h)
+            neg_max = sb.tile([P, 1], F32, name="neg_max%d" % h)
+            row_sum = sb.tile([P, 1], F32, name="row_sum%d" % h)
+            inv_sum = sb.tile([P, 1], F32, name="inv_sum%d" % h)
+            prob = sb.tile([P, I], F32, name="prob%d" % h)
+            w_bf = sb.tile([P, I], BF16, name="w_bf%d" % h)
+            nc.tensor.matmul_mx(
+                out=scores[:], lhsT=q_codes[:, cols].bitcast(FP8X4), lhsT_scale=q_scales[:, cols],
+                rhs=k_words[:].bitcast(FP4X4), rhs_scale=k_bytes[:], start=True, stop=True,
+            )
+            nc.vector.tensor_reduce(neg_max[:], scores[:], AXIS.X, ALU.max, negate=True)
+            nc.scalar.activation(prob[:], scores[:], ACT.Exp, bias=neg_max[:], accum_out=row_sum[:])
+            nc.vector.reciprocal(inv_sum[:], row_sum[:])
+            nc.vector.scalar_tensor_tensor(
+                w_bf[:].rearrange("q (p t) -> q p t", t=PACK), prob[:].rearrange("q (p t) -> q p t", t=PACK),
+                inv_sum[:], size_rows[:].rearrange("q t p -> q p t"), ALU.mult, ALU.mult,
+            )
+            w_pairs = w_bf[:].bitcast(F32)
+            for u in range(2):
+                nc.tensor.transpose(w_turned[:, h, u, :], w_pairs[:, u : I // 2 : 2], ident[:])
+        w_in = sb.tile([P, Q * PACK], BF16, align_bytes=64)
+        w_codes = sb.tile([P, Q], U32, align_bytes=64)
+        w_scales = sb.tile([P, Q], U8, align_bytes=64)
+        nc.scalar.copy(
+            w_in[:].bitcast(F32).rearrange("p (h q u) -> p h q u", h=HALVES, u=2),
+            w_turned[:].rearrange("p h u q -> p h q u"),
+        )
+        nc.vector.quantize_mx(w_codes[:].bitcast(FP8X4), w_scales[:], w_in[:])
+
+        reads = [ps.tile([P, 2, Q], F32, name="reads%d" % b) for b in range(TILES // 2)]
+        for j in range(TILES):
+            v_bf = sb.tile([P, I], BF16, name="v_bf%d" % j)
+            v_in = sb.tile([P, P * PACK], BF16, name="v_in%d" % j, align_bytes=64)
+            v_codes = sb.tile([P, P], U32, name="v_codes%d" % j, align_bytes=64)
+            v_scales = sb.tile([P, P], U8, name="v_scales%d" % j, align_bytes=64)
+            v_turned = ps_turn.tile([P, 2, P], F32)
+            nc.vector.tensor_copy(v_bf[:], val_pool[j][:].indirect(slots[:]))
+            v_pairs = v_bf[:].bitcast(F32)
+            for u in range(2):
+                nc.tensor.transpose(v_turned[:, u, :], v_pairs[:, u : I // 2 : 2], ident[:])
+            nc.scalar.copy(
+                v_in[:].bitcast(F32).rearrange("p (e u) -> p e u", u=2), v_turned[:].rearrange("p u e -> p e u")
+            )
+            nc.vector.quantize_mx(v_codes[:].bitcast(FP8X4), v_scales[:], v_in[:])
+            nc.tensor.matmul_mx(
+                out=reads[j // 2][:, j % 2, :], lhsT=v_codes[:].bitcast(FP8X4), lhsT_scale=v_scales[:],
+                rhs=w_codes[:].bitcast(FP8X4), rhs_scale=w_scales[:], start=True, stop=True,
+            )
+
+        neg_ff = sb.tile([P, TILES], F32)
+        nc.scalar.activation(neg_ff[:], ff_cols[:], ACT.Copy, scale=-1.0 / J)
+        out_by_tile = out.rearrange("(p j) q -> p j q", j=TILES)
+        first = sb.tile([P, TILES - 1, Q], F32)
+        last = sb.tile([P, Q], F32)
+        for j in range(TILES):
+            picked = sb.tile([P, J], F32, name="picked%d" % j)
+            scaled = sb.tile([P, J], F32, name="scaled%d" % j)
+            neg_mb = sb.tile([P, 1], F32, name="neg_mb%d" % j)
+            nc.vector.tensor_copy(picked[:], back_pool[j][:].indirect(slots2[:]))
+            nc.scalar.activation(scaled[:], picked[:], ACT.Copy, scale=neg_ff[:, j : j + 1], accum_out=neg_mb[:])
+            result = first[:, j, :] if j < TILES - 1 else last[:]
+            nc.scalar.activation(result, reads[j // 2][:, j % 2, :], ACT.Identity, bias=neg_mb[:])
+        nc.sync.dma_start(out_by_tile[:, : TILES - 1, :], first[:])
+        nc.sync.dma_start(out_by_tile[:, TILES - 1, :], last[:])

@@ -31,114 +31,139 @@ def tile_attend_relativeread_kernel(tc, query, keys_words, keys_scales, size, va
         ps = ctx.enter_context(tc.psum_pool(name="ps", bufs=1))
         ps_turn = ctx.enter_context(tc.psum_pool(name="ps_turn", bufs=2))
 
+        def placed(shape, dtype, name, place):
+            return sb.tile(shape, dtype, name=name, tag=place, align_bytes=64)
+
         slots = sb.tile([P, I // 16], U16)
         slots2 = sb.tile([P, J // 16], U16)
-        key_words = sb.tile([P, T], U16, align_bytes=64)
-        key_bytes = sb.tile([P, T], U8, align_bytes=64)
+        key_words = sb.tile([P, T], U16)
+        key_bytes = sb.tile([P, T], U8)
         q_raw = sb.tile([P, PACK, Q], F32)
         size_cols = sb.tile([P, PACK], F32)
         ff_cols = sb.tile([P, TILES], F32)
-        val_pool = [sb.tile([P, T], F32, name="val_pool%d" % j) for j in range(TILES)]
-        back_pool = [sb.tile([P, U], F32, name="back_pool%d" % j) for j in range(TILES)]
+        val_pool = [placed([P, T], F32, "val_pool%d" % j, "vals%d" % j) for j in range(TILES)]
+        back_pool = [placed([P, U], F32, "back_pool%d" % j, "back%d" % j) for j in range(TILES)]
         ident = sb.tile([P, P], F32)
 
         nc.gpsimd.memset(key_bytes[:].bitcast(I32), 0)
+        make_identity(nc, ident[:])
         vals_by_tile = vals.rearrange("(p j) t -> j p t", j=TILES)
         back_by_tile = back.rearrange("(p j) u -> j p u", j=TILES)
-        nc.gpsimd.dma_start(size_cols[:], size.rearrange("o (p t) -> p (o t)", t=PACK))
         nc.sync.dma_start(key_words[:].bitcast(I32), keys_words[0].bitcast(I32))
         nc.sync.dma_start(slots[:], offs)
-        nc.sync.dma_start(q_raw[:], query.rearrange("(p t) q -> p t q", t=PACK))
         for r in range(4):
             nc.sync.dma_start(
                 key_bytes[32 * r : 32 * r + 4, :].bitcast(I32), keys_scales[0, 4 * r : 4 * r + 4, :].bitcast(I32)
             )
-        for j in range(TILES - 1):
+        nc.sync.dma_start(q_raw[:], query.rearrange("(p t) q -> p t q", t=PACK))
+        nc.sync.dma_start(val_pool[0][:], vals_by_tile[0])
+        nc.sync.dma_start(size_cols[:], size.rearrange("o (p t) -> p (o t)", t=PACK))
+        for j in range(1, TILES):
             nc.sync.dma_start(val_pool[j][:], vals_by_tile[j])
         nc.sync.dma_start(slots2[:], offs2)
         nc.sync.dma_start(ff_cols[:], ff.rearrange("(p j) o -> p (j o)", j=TILES))
-        nc.sync.dma_start(val_pool[TILES - 1][:], vals_by_tile[TILES - 1])
         for j in range(TILES):
             nc.sync.dma_start(back_pool[j][:], back_by_tile[j])
-        make_identity(nc, ident[:])
 
-        k_words = sb.tile([P, I], U16, align_bytes=64)
+        k_words = placed([P, I], U16, "k_words", "gathered0")
         k_bytes = sb.tile([P, I], U8, align_bytes=64)
         nc.vector.tensor_copy(k_words[:], key_words[:].indirect(slots[:]))
         nc.vector.tensor_copy(k_bytes[:], key_bytes[:].indirect(slots[:]))
 
-        q_bf = sb.tile([P, Q, PACK], BF16, align_bytes=64)
-        q_codes = sb.tile([P, Q], U32, align_bytes=64)
-        q_scales = sb.tile([P, Q], U8, align_bytes=64)
-        nc.scalar.copy(q_bf[:], q_raw[:].rearrange("p t q -> p q t"))
-        nc.vector.quantize_mx(q_codes[:].bitcast(FP8X4), q_scales[:], q_bf[:].rearrange("p q t -> p (q t)"))
+        scores = []
+        for h in range(HALVES):
+            q_bf = sb.tile([P, P, PACK], BF16, name="q_bf%d" % h, align_bytes=64)
+            q_codes = sb.tile([P, P], U32, name="q_codes%d" % h, align_bytes=64)
+            q_scales = sb.tile([P, P], U8, name="q_scales%d" % h, align_bytes=64)
+            nc.scalar.copy(q_bf[:], q_raw[:, :, h * P : (h + 1) * P].rearrange("p t q -> p q t"))
+            nc.vector.quantize_mx(q_codes[:].bitcast(FP8X4), q_scales[:], q_bf[:].rearrange("p q t -> p (q t)"))
+            scores.append(ps.tile([P, I], F32, name="scores%d" % h))
+            nc.tensor.matmul_mx(
+                out=scores[h][:], lhsT=q_codes[:].bitcast(FP8X4), lhsT_scale=q_scales[:],
+                rhs=k_words[:].bitcast(FP4X4), rhs_scale=k_bytes[:], start=True, stop=True,
+            )
 
         size_rows = ps.tile([P, PACK, P], F32)
         for t in range(PACK):
             nc.tensor.transpose(size_rows[:, t, :], size_cols[:, t : t + 1].to_broadcast([P, P]), ident[:])
 
-        w_turned = ps.tile([P, HALVES, 2, P], F32)
-        for h in range(HALVES):
-            cols = slice(h * P, (h + 1) * P)
-            scores = ps.tile([P, I], F32, name="scores%d" % h)
-            neg_max = sb.tile([P, 1], F32, name="neg_max%d" % h)
-            row_sum = sb.tile([P, 1], F32, name="row_sum%d" % h)
-            inv_sum = sb.tile([P, 1], F32, name="inv_sum%d" % h)
-            prob = sb.tile([P, I], F32, name="prob%d" % h)
-            w_bf = sb.tile([P, I], BF16, name="w_bf%d" % h)
-            nc.tensor.matmul_mx(
-                out=scores[:], lhsT=q_codes[:, cols].bitcast(FP8X4), lhsT_scale=q_scales[:, cols],
-                rhs=k_words[:].bitcast(FP4X4), rhs_scale=k_bytes[:], start=True, stop=True,
-            )
-            nc.vector.tensor_reduce(neg_max[:], scores[:], AXIS.X, ALU.max, negate=True)
-            nc.scalar.activation(prob[:], scores[:], ACT.Exp, bias=neg_max[:], accum_out=row_sum[:])
-            nc.vector.reciprocal(inv_sum[:], row_sum[:])
-            nc.vector.scalar_tensor_tensor(
-                w_bf[:].rearrange("q (p t) -> q p t", t=PACK), prob[:].rearrange("q (p t) -> q p t", t=PACK),
-                inv_sum[:], size_rows[:].rearrange("q t p -> q p t"), ALU.mult, ALU.mult,
-            )
-            w_pairs = w_bf[:].bitcast(F32)
-            for u in range(2):
-                nc.tensor.transpose(w_turned[:, h, u, :], w_pairs[:, u : I // 2 : 2], ident[:])
-        w_in = sb.tile([P, Q * PACK], BF16, align_bytes=64)
-        w_codes = sb.tile([P, Q], U32, align_bytes=64)
-        w_scales = sb.tile([P, Q], U8, align_bytes=64)
-        nc.scalar.copy(
-            w_in[:].bitcast(F32).rearrange("p (h q u) -> p h q u", h=HALVES, u=2),
-            w_turned[:].rearrange("p h u q -> p h q u"),
-        )
-        nc.vector.quantize_mx(w_codes[:].bitcast(FP8X4), w_scales[:], w_in[:])
-
-        reads = [ps.tile([P, 2, Q], F32, name="reads%d" % b) for b in range(TILES // 2)]
-        for j in range(TILES):
-            v_bf = sb.tile([P, I], BF16, name="v_bf%d" % j)
-            v_in = sb.tile([P, P * PACK], BF16, name="v_in%d" % j, align_bytes=64)
-            v_codes = sb.tile([P, P], U32, name="v_codes%d" % j, align_bytes=64)
-            v_scales = sb.tile([P, P], U8, name="v_scales%d" % j, align_bytes=64)
+        def gather_and_turn(j, v_in):
+            v_bf = placed([P, I], BF16, "v_bf%d" % j, "gathered%d" % j)
             v_turned = ps_turn.tile([P, 2, P], F32)
             nc.vector.tensor_copy(v_bf[:], val_pool[j][:].indirect(slots[:]))
             v_pairs = v_bf[:].bitcast(F32)
             for u in range(2):
                 nc.tensor.transpose(v_turned[:, u, :], v_pairs[:, u : I // 2 : 2], ident[:])
             nc.scalar.copy(
-                v_in[:].bitcast(F32).rearrange("p (e u) -> p e u", u=2), v_turned[:].rearrange("p u e -> p e u")
-            )
-            nc.vector.quantize_mx(v_codes[:].bitcast(FP8X4), v_scales[:], v_in[:])
-            nc.tensor.matmul_mx(
-                out=reads[j // 2][:, j % 2, :], lhsT=v_codes[:].bitcast(FP8X4), lhsT_scale=v_scales[:],
-                rhs=w_codes[:].bitcast(FP8X4), rhs_scale=w_scales[:], start=True, stop=True,
+                v_in[:, (j % 2) * I : (j % 2 + 1) * I].bitcast(F32).rearrange("p (e u) -> p e u", u=2),
+                v_turned[:].rearrange("p u e -> p e u"),
             )
 
+        def gather_background(j):
+            picked = sb.tile([P, J], F32, name="picked%d" % j)
+            nc.vector.tensor_copy(picked[:], back_pool[j][:].indirect(slots2[:]))
+            return picked
+
+        def quantise_pair(b, v_in, place):
+            v_codes = placed([P, 2 * P], U32, "v_codes%d" % b, place)
+            v_scales = sb.tile([P, 2 * P], U8, name="v_scales%d" % b, align_bytes=64)
+            nc.vector.quantize_mx(v_codes[:].bitcast(FP8X4), v_scales[:], v_in[:])
+            reads = ps.tile([P, 2, Q], F32, name="reads%d" % b)
+            for a in range(2):
+                cols = slice(a * P, (a + 1) * P)
+                nc.tensor.matmul_mx(
+                    out=reads[:, a, :], lhsT=v_codes[:, cols].bitcast(FP8X4), lhsT_scale=v_scales[:, cols],
+                    rhs=w_codes[:].bitcast(FP8X4), rhs_scale=w_scales[:], start=True, stop=True,
+                )
+            return reads, v_codes
+
+        v_ins = [sb.tile([P, 2 * I], BF16, name="v_in%d" % b, align_bytes=64) for b in range(TILES // 2)]
+
+        row_sum = sb.tile([P, HALVES], F32)
+        prob = []
+        for h in range(HALVES):
+            neg_max = sb.tile([P, 1], F32, name="neg_max%d" % h)
+            prob.append(sb.tile([P, I], F32, name="prob%d" % h))
+            nc.vector.tensor_reduce(neg_max[:], scores[h][:], AXIS.X, ALU.max, negate=True)
+            nc.scalar.activation(prob[h][:], scores[h][:], ACT.Exp, bias=neg_max[:], accum_out=row_sum[:, h : h + 1])
+        gather_and_turn(0, v_ins[0])
+        inv_sum = placed([P, HALVES], F32, "inv_sum", "vals0")
+        nc.vector.reciprocal(inv_sum[:], row_sum[:])
+        w_turned = ps.tile([P, HALVES, 2, P], F32)
+        for h in range(HALVES):
+            w_bf = sb.tile([P, I], BF16, name="w_bf%d" % h)
+            nc.vector.scalar_tensor_tensor(
+                w_bf[:].rearrange("q (p t) -> q p t", t=PACK), prob[h][:].rearrange("q (p t) -> q p t", t=PACK),
+                inv_sum[:, h : h + 1], size_rows[:].rearrange("q t p -> q p t"), ALU.mult, ALU.mult,
+            )
+            w_pairs = w_bf[:].bitcast(F32)
+            for u in range(2):
+                nc.tensor.transpose(w_turned[:, h, u, :], w_pairs[:, u : I // 2 : 2], ident[:])
+        w_in = sb.tile([P, Q * PACK], BF16, align_bytes=64)
+        nc.scalar.copy(
+            w_in[:].bitcast(F32).rearrange("p (h q u) -> p h q u", h=HALVES, u=2),
+            w_turned[:].rearrange("p h u q -> p h q u"),
+        )
+        gather_and_turn(1, v_ins[0])
+        w_codes = placed([P, Q], U32, "w_codes", "vals1")
+        w_scales = sb.tile([P, Q], U8, align_bytes=64)
+        nc.vector.quantize_mx(w_codes[:].bitcast(FP8X4), w_scales[:], w_in[:])
+        gather_and_turn(2, v_ins[1])
+        reads0, codes0 = quantise_pair(0, v_ins[0], "vals2")
+        gather_and_turn(3, v_ins[1])
+        early = [gather_background(j) for j in range(2)]
+        reads1, codes1 = quantise_pair(1, v_ins[1], "back1")
+        reads = [reads0, reads1]
+
         neg_ff = sb.tile([P, TILES], F32)
-        nc.scalar.activation(neg_ff[:], ff_cols[:], ACT.Copy, scale=-1.0 / J)
+        nc.gpsimd.tensor_scalar(neg_ff[:], ff_cols[:], -1.0 / J, None, ALU.mult)
         out_by_tile = out.rearrange("(p j) q -> p j q", j=TILES)
         first = sb.tile([P, TILES - 1, Q], F32)
         last = sb.tile([P, Q], F32)
         for j in range(TILES):
-            picked = sb.tile([P, J], F32, name="picked%d" % j)
+            picked = early[j] if j < 2 else gather_background(j)
             scaled = sb.tile([P, J], F32, name="scaled%d" % j)
             neg_mb = sb.tile([P, 1], F32, name="neg_mb%d" % j)
-            nc.vector.tensor_copy(picked[:], back_pool[j][:].indirect(slots2[:]))
             nc.scalar.activation(scaled[:], picked[:], ACT.Copy, scale=neg_ff[:, j : j + 1], accum_out=neg_mb[:])
             result = first[:, j, :] if j < TILES - 1 else last[:]
             nc.scalar.activation(result, reads[j // 2][:, j % 2, :], ACT.Identity, bias=neg_mb[:])

@@ -49,16 +49,15 @@ def tile_attend_relativeread_kernel(tc, query, keys_words, keys_scales, size, va
         make_identity(nc, ident[:])
         vals_by_tile = vals.rearrange("(p j) t -> j p t", j=TILES)
         back_by_tile = back.rearrange("(p j) u -> j p u", j=TILES)
-        nc.sync.dma_start(key_words[:].bitcast(I32), keys_words[0].bitcast(I32))
         nc.sync.dma_start(slots[:], offs)
+        nc.sync.dma_start(key_words[:].bitcast(I32), keys_words[0].bitcast(I32))
         for r in range(4):
             nc.sync.dma_start(
-                key_bytes[32 * r : 32 * r + 4, :].bitcast(I32), keys_scales[0, 4 * r : 4 * r + 4, :].bitcast(I32)
+                key_bytes[r:P:32, :].bitcast(I32), keys_scales[0, r:16:4, :].bitcast(I32)
             )
-        nc.sync.dma_start(q_raw[:], query.rearrange("(p t) q -> p t q", t=PACK))
-        nc.sync.dma_start(val_pool[0][:], vals_by_tile[0])
         nc.sync.dma_start(size_cols[:], size.rearrange("o (p t) -> p (o t)", t=PACK))
-        for j in range(1, TILES):
+        nc.sync.dma_start(q_raw[:], query.rearrange("(p t) q -> p t q", t=PACK))
+        for j in range(TILES):
             nc.sync.dma_start(val_pool[j][:], vals_by_tile[j])
         nc.sync.dma_start(slots2[:], offs2)
         nc.sync.dma_start(ff_cols[:], ff.rearrange("(p j) o -> p (j o)", j=TILES))
@@ -87,17 +86,17 @@ def tile_attend_relativeread_kernel(tc, query, keys_words, keys_scales, size, va
         for t in range(PACK):
             nc.tensor.transpose(size_rows[:, t, :], size_cols[:, t : t + 1].to_broadcast([P, P]), ident[:])
 
-        def gather_and_turn(j, v_in):
+        def gather_values(j):
             v_bf = placed([P, I], BF16, "v_bf%d" % j, "gathered%d" % j)
-            v_turned = ps_turn.tile([P, 2, P], F32)
             nc.vector.tensor_copy(v_bf[:], val_pool[j][:].indirect(slots[:]))
+            return v_bf
+
+        def turn_values(v_bf, v_in):
+            v_turned = ps_turn.tile([P, 2, P], F32)
             v_pairs = v_bf[:].bitcast(F32)
             for u in range(2):
                 nc.tensor.transpose(v_turned[:, u, :], v_pairs[:, u : I // 2 : 2], ident[:])
-            nc.scalar.copy(
-                v_in[:, (j % 2) * I : (j % 2 + 1) * I].bitcast(F32).rearrange("p (e u) -> p e u", u=2),
-                v_turned[:].rearrange("p u e -> p e u"),
-            )
+            nc.scalar.copy(v_in.bitcast(F32).rearrange("p (e u) -> p e u", u=2), v_turned[:].rearrange("p u e -> p e u"))
 
         def gather_background(j):
             picked = sb.tile([P, J], F32, name="picked%d" % j)
@@ -107,7 +106,7 @@ def tile_attend_relativeread_kernel(tc, query, keys_words, keys_scales, size, va
         def quantise_pair(b, v_in, place):
             v_codes = placed([P, 2 * P], U32, "v_codes%d" % b, place)
             v_scales = sb.tile([P, 2 * P], U8, name="v_scales%d" % b, align_bytes=64)
-            nc.vector.quantize_mx(v_codes[:].bitcast(FP8X4), v_scales[:], v_in[:])
+            nc.vector.quantize_mx(v_codes[:].bitcast(FP8X4), v_scales[:], v_in)
             reads = ps.tile([P, 2, Q], F32, name="reads%d" % b)
             for a in range(2):
                 cols = slice(a * P, (a + 1) * P)
@@ -115,9 +114,7 @@ def tile_attend_relativeread_kernel(tc, query, keys_words, keys_scales, size, va
                     out=reads[:, a, :], lhsT=v_codes[:, cols].bitcast(FP8X4), lhsT_scale=v_scales[:, cols],
                     rhs=w_codes[:].bitcast(FP8X4), rhs_scale=w_scales[:], start=True, stop=True,
                 )
-            return reads, v_codes
-
-        v_ins = [sb.tile([P, 2 * I], BF16, name="v_in%d" % b, align_bytes=64) for b in range(TILES // 2)]
+            return reads
 
         row_sum = sb.tile([P, HALVES], F32)
         prob = []
@@ -126,7 +123,14 @@ def tile_attend_relativeread_kernel(tc, query, keys_words, keys_scales, size, va
             prob.append(sb.tile([P, I], F32, name="prob%d" % h))
             nc.vector.tensor_reduce(neg_max[:], scores[h][:], AXIS.X, ALU.max, negate=True)
             nc.scalar.activation(prob[h][:], scores[h][:], ACT.Exp, bias=neg_max[:], accum_out=row_sum[:, h : h + 1])
-        gather_and_turn(0, v_ins[0])
+        v_bf0 = gather_values(0)
+        val_pool1_bf = sb.tile([P, T], BF16)
+        nc.scalar.activation(val_pool1_bf[:], val_pool[1][:], ACT.Copy)
+        staged = placed([P, Q * PACK + 2 * I], BF16, "staged", "vals1")
+        w_in = staged[:, : Q * PACK]
+        even_in = staged[:, Q * PACK :]
+        odd_in = sb.tile([P, 2 * I], BF16, align_bytes=64)
+        turn_values(v_bf0, even_in[:, :I])
         inv_sum = placed([P, HALVES], F32, "inv_sum", "vals0")
         nc.vector.reciprocal(inv_sum[:], row_sum[:])
         w_turned = ps.tile([P, HALVES, 2, P], F32)
@@ -139,33 +143,47 @@ def tile_attend_relativeread_kernel(tc, query, keys_words, keys_scales, size, va
             w_pairs = w_bf[:].bitcast(F32)
             for u in range(2):
                 nc.tensor.transpose(w_turned[:, h, u, :], w_pairs[:, u : I // 2 : 2], ident[:])
-        w_in = sb.tile([P, Q * PACK], BF16, align_bytes=64)
         nc.scalar.copy(
-            w_in[:].bitcast(F32).rearrange("p (h q u) -> p h q u", h=HALVES, u=2),
+            w_in.bitcast(F32).rearrange("p (h q u) -> p h q u", h=HALVES, u=2),
             w_turned[:].rearrange("p h u q -> p h q u"),
         )
-        gather_and_turn(1, v_ins[0])
-        w_codes = placed([P, Q], U32, "w_codes", "vals1")
+        v_bf1 = sb.tile([P, I], BF16)
+        nc.scalar.activation(v_bf1[:], val_pool1_bf[:].indirect(slots[:]), ACT.Copy)
+        turn_values(gather_values(2), even_in[:, I:])
+        w_codes = placed([P, Q], U32, "w_codes", "vals2")
         w_scales = sb.tile([P, Q], U8, align_bytes=64)
-        nc.vector.quantize_mx(w_codes[:].bitcast(FP8X4), w_scales[:], w_in[:])
-        gather_and_turn(2, v_ins[1])
-        reads0, codes0 = quantise_pair(0, v_ins[0], "vals2")
-        gather_and_turn(3, v_ins[1])
-        early = [gather_background(j) for j in range(2)]
-        reads1, codes1 = quantise_pair(1, v_ins[1], "back1")
-        reads = [reads0, reads1]
+        nc.vector.quantize_mx(w_codes[:].bitcast(FP8X4), w_scales[:], w_in)
+        turn_values(v_bf1, odd_in[:, :I])
+        turn_values(gather_values(3), odd_in[:, I:])
+        reads_even = quantise_pair(0, even_in, "vals3")
+        early = [gather_background(0)]
+        reads_odd = quantise_pair(1, odd_in[:], "back0")
+        reads = [reads_even, reads_odd]
 
         neg_ff = sb.tile([P, TILES], F32)
         nc.gpsimd.tensor_scalar(neg_ff[:], ff_cols[:], -1.0 / J, None, ALU.mult)
         out_by_tile = out.rearrange("(p j) q -> p j q", j=TILES)
-        first = sb.tile([P, TILES - 1, Q], F32)
-        last = sb.tile([P, Q], F32)
-        for j in range(TILES):
-            picked = early[j] if j < 2 else gather_background(j)
-            scaled = sb.tile([P, J], F32, name="scaled%d" % j)
-            neg_mb = sb.tile([P, 1], F32, name="neg_mb%d" % j)
+        result = sb.tile([P, TILES - 1, Q], F32)
+
+        def sum_background(name, picked, j):
+            scaled = sb.tile([P, picked.shape[1]], F32, name="scaled" + name)
+            neg_mb = sb.tile([P, 1], F32, name="neg_mb" + name)
             nc.scalar.activation(scaled[:], picked[:], ACT.Copy, scale=neg_ff[:, j : j + 1], accum_out=neg_mb[:])
-            result = first[:, j, :] if j < TILES - 1 else last[:]
-            nc.scalar.activation(result, reads[j // 2][:, j % 2, :], ACT.Identity, bias=neg_mb[:])
-        nc.sync.dma_start(out_by_tile[:, : TILES - 1, :], first[:])
-        nc.sync.dma_start(out_by_tile[:, TILES - 1, :], last[:])
+            return neg_mb
+
+        for j in range(TILES - 1):
+            picked = early[j] if j < 1 else gather_background(j)
+            neg_mb = sum_background(str(j), picked, j)
+            nc.scalar.activation(result[:, j, :], reads[j % 2][:, j // 2, :], ACT.Identity, bias=neg_mb[:])
+            if j > 0:
+                done = slice(0, 2) if j == 1 else slice(2, 3)
+                nc.sync.dma_start(out_by_tile[:, done, :], result[:, done, :])
+        j = TILES - 1
+        parts = []
+        for a in range(2):
+            picked = sb.tile([P, J // 2], F32, name="picked_last%d" % a)
+            nc.vector.tensor_copy(picked[:], back_pool[j][:].indirect(slots2[:, a * J // 32 : (a + 1) * J // 32]))
+            parts.append(sum_background("_last%d" % a, picked, j))
+        last = sb.tile([P, Q], F32)
+        nc.vector.tensor_scalar(last[:], reads[j % 2][:, j // 2, :], parts[0][:], parts[1][:], ALU.add, ALU.add)
+        nc.sync.dma_start(out_by_tile[:, j, :], last[:])

@@ -20,8 +20,13 @@ AXIS = mybir.AxisListType
 
 P = 128
 PACK = 4
+QUADRANT = 32
+PER_COLUMN = 16
+LINE = 4
+MX_ALIGN = 64
 HALVES = Q // P
 TILES = E // P
+FEATURE_TILE_OF_POOL = (0, 2, 1, 3)
 
 
 def tile_attend_relativeread_kernel(tc, query, keys_words, keys_scales, size, vals, back, ff, offs, offs2, out):
@@ -32,16 +37,16 @@ def tile_attend_relativeread_kernel(tc, query, keys_words, keys_scales, size, va
         ps_turn = ctx.enter_context(tc.psum_pool(name="ps_turn", bufs=2))
 
         def placed(shape, dtype, name, place):
-            return sb.tile(shape, dtype, name=name, tag=place, align_bytes=64)
+            return sb.tile(shape, dtype, name=name, tag=place, align_bytes=MX_ALIGN)
 
-        slots = sb.tile([P, I // 16], U16)
-        slots2 = sb.tile([P, J // 16], U16)
+        slots = sb.tile([P, I // PER_COLUMN], U16)
+        slots2 = sb.tile([P, J // PER_COLUMN], U16)
         key_words = sb.tile([P, T], U16)
         key_bytes = sb.tile([P, T], U8)
-        q_raw = sb.tile([P, PACK, Q], F32)
+        q_raw = placed([P, PACK, Q], F32, "q_raw", "queries")
         size_cols = sb.tile([P, PACK], F32)
         ff_cols = sb.tile([P, TILES], F32)
-        val_pool = [placed([P, T], F32, "val_pool%d" % j, "vals%d" % j) for j in range(TILES)]
+        val_pool = [placed([P, T], F32, "val_pool%d" % n, "vals%d" % n) for n in range(TILES)]
         back_pool = [placed([P, U], F32, "back_pool%d" % j, "back%d" % j) for j in range(TILES)]
         ident = sb.tile([P, P], F32)
 
@@ -49,32 +54,36 @@ def tile_attend_relativeread_kernel(tc, query, keys_words, keys_scales, size, va
         make_identity(nc, ident[:])
         vals_by_tile = vals.rearrange("(p j) t -> j p t", j=TILES)
         back_by_tile = back.rearrange("(p j) u -> j p u", j=TILES)
+        rows = P // QUADRANT
         nc.sync.dma_start(slots[:], offs)
         nc.sync.dma_start(key_words[:].bitcast(I32), keys_words[0].bitcast(I32))
-        for r in range(4):
+        for r in range(rows):
             nc.sync.dma_start(
-                key_bytes[r:P:32, :].bitcast(I32), keys_scales[0, r:16:4, :].bitcast(I32)
+                key_bytes[r:P:QUADRANT, :].bitcast(I32), keys_scales[0, r : rows * rows : rows, :].bitcast(I32)
             )
         nc.sync.dma_start(size_cols[:], size.rearrange("o (p t) -> p (o t)", t=PACK))
         nc.sync.dma_start(q_raw[:], query.rearrange("(p t) q -> p t q", t=PACK))
-        for j in range(TILES):
-            nc.sync.dma_start(val_pool[j][:], vals_by_tile[j])
+        for n in range(TILES):
+            nc.sync.dma_start(val_pool[n][:], vals_by_tile[FEATURE_TILE_OF_POOL[n]])
         nc.sync.dma_start(slots2[:], offs2)
         nc.sync.dma_start(ff_cols[:], ff.rearrange("(p j) o -> p (j o)", j=TILES))
         for j in range(TILES):
             nc.sync.dma_start(back_pool[j][:], back_by_tile[j])
 
         k_words = placed([P, I], U16, "k_words", "gathered0")
-        k_bytes = sb.tile([P, I], U8, align_bytes=64)
+        k_bytes = sb.tile([P, I], U8, align_bytes=MX_ALIGN)
         nc.vector.tensor_copy(k_words[:], key_words[:].indirect(slots[:]))
         nc.vector.tensor_copy(k_bytes[:], key_bytes[:].indirect(slots[:]))
 
         scores = []
         for h in range(HALVES):
-            q_bf = sb.tile([P, P, PACK], BF16, name="q_bf%d" % h, align_bytes=64)
-            q_codes = sb.tile([P, P], U32, name="q_codes%d" % h, align_bytes=64)
-            q_scales = sb.tile([P, P], U8, name="q_scales%d" % h, align_bytes=64)
-            nc.scalar.copy(q_bf[:], q_raw[:, :, h * P : (h + 1) * P].rearrange("p t q -> p q t"))
+            q_bf = sb.tile([P, P, PACK], BF16, name="q_bf%d" % h, align_bytes=MX_ALIGN)
+            q_codes = sb.tile([P, P], U32, name="q_codes%d" % h, align_bytes=MX_ALIGN)
+            q_scales = sb.tile([P, P], U8, name="q_scales%d" % h, align_bytes=MX_ALIGN)
+            nc.scalar.copy(
+                q_bf[:].rearrange("p (c i) t -> p c t i", i=LINE),
+                q_raw[:, :, h * P : (h + 1) * P].rearrange("p t (c i) -> p c t i", i=LINE),
+            )
             nc.vector.quantize_mx(q_codes[:].bitcast(FP8X4), q_scales[:], q_bf[:].rearrange("p q t -> p (q t)"))
             scores.append(ps.tile([P, I], F32, name="scores%d" % h))
             nc.tensor.matmul_mx(
@@ -82,20 +91,25 @@ def tile_attend_relativeread_kernel(tc, query, keys_words, keys_scales, size, va
                 rhs=k_words[:].bitcast(FP4X4), rhs_scale=k_bytes[:], start=True, stop=True,
             )
 
-        size_rows = ps.tile([P, PACK, P], F32)
+        size_turned = ps.tile([P, PACK, P], F32)
         for t in range(PACK):
-            nc.tensor.transpose(size_rows[:, t, :], size_cols[:, t : t + 1].to_broadcast([P, P]), ident[:])
+            nc.tensor.transpose(size_turned[:, t, :], size_cols[:, t : t + 1].to_broadcast([P, P]), ident[:])
+        size_row = placed([P, I], F32, "size_row", "queries")
+        nc.scalar.copy(size_row[:].rearrange("q (p t) -> q p t", t=PACK), size_turned[:].rearrange("q t p -> q p t"))
 
-        def gather_values(j):
-            v_bf = placed([P, I], BF16, "v_bf%d" % j, "gathered%d" % j)
-            nc.vector.tensor_copy(v_bf[:], val_pool[j][:].indirect(slots[:]))
+        def gather_values(n):
+            v_bf = placed([P, I], BF16, "v_bf%d" % n, "gathered%d" % n)
+            nc.vector.tensor_copy(v_bf[:], val_pool[n][:].indirect(slots[:]))
             return v_bf
+
+        def turn_pairs(turned, by_slot):
+            pairs = by_slot[:].bitcast(F32)
+            for u in range(2):
+                nc.tensor.transpose(turned[:, u, :], pairs[:, u : I // 2 : 2], ident[:])
 
         def turn_values(v_bf, v_in):
             v_turned = ps_turn.tile([P, 2, P], F32)
-            v_pairs = v_bf[:].bitcast(F32)
-            for u in range(2):
-                nc.tensor.transpose(v_turned[:, u, :], v_pairs[:, u : I // 2 : 2], ident[:])
+            turn_pairs(v_turned[:], v_bf)
             nc.scalar.copy(v_in.bitcast(F32).rearrange("p (e u) -> p e u", u=2), v_turned[:].rearrange("p u e -> p e u"))
 
         def gather_background(j):
@@ -103,18 +117,18 @@ def tile_attend_relativeread_kernel(tc, query, keys_words, keys_scales, size, va
             nc.vector.tensor_copy(picked[:], back_pool[j][:].indirect(slots2[:]))
             return picked
 
-        def quantise_pair(b, v_in, place):
+        def read_pair(b, v_in, place):
             v_codes = placed([P, 2 * P], U32, "v_codes%d" % b, place)
-            v_scales = sb.tile([P, 2 * P], U8, name="v_scales%d" % b, align_bytes=64)
+            v_scales = sb.tile([P, 2 * P], U8, name="v_scales%d" % b, align_bytes=MX_ALIGN)
             nc.vector.quantize_mx(v_codes[:].bitcast(FP8X4), v_scales[:], v_in)
-            reads = ps.tile([P, 2, Q], F32, name="reads%d" % b)
+            bank = ps.tile([P, 2, Q], F32, name="reads%d" % b)
             for a in range(2):
                 cols = slice(a * P, (a + 1) * P)
                 nc.tensor.matmul_mx(
-                    out=reads[:, a, :], lhsT=v_codes[:, cols].bitcast(FP8X4), lhsT_scale=v_scales[:, cols],
+                    out=bank[:, a, :], lhsT=v_codes[:, cols].bitcast(FP8X4), lhsT_scale=v_scales[:, cols],
                     rhs=w_codes[:].bitcast(FP8X4), rhs_scale=w_scales[:], start=True, stop=True,
                 )
-            return reads
+            return bank
 
         row_sum = sb.tile([P, HALVES], F32)
         prob = []
@@ -123,67 +137,72 @@ def tile_attend_relativeread_kernel(tc, query, keys_words, keys_scales, size, va
             prob.append(sb.tile([P, I], F32, name="prob%d" % h))
             nc.vector.tensor_reduce(neg_max[:], scores[h][:], AXIS.X, ALU.max, negate=True)
             nc.scalar.activation(prob[h][:], scores[h][:], ACT.Exp, bias=neg_max[:], accum_out=row_sum[:, h : h + 1])
+
         v_bf0 = gather_values(0)
         val_pool1_bf = sb.tile([P, T], BF16)
         nc.scalar.activation(val_pool1_bf[:], val_pool[1][:], ACT.Copy)
         staged = placed([P, Q * PACK + 2 * I], BF16, "staged", "vals1")
         w_in = staged[:, : Q * PACK]
-        even_in = staged[:, Q * PACK :]
-        odd_in = sb.tile([P, 2 * I], BF16, align_bytes=64)
-        turn_values(v_bf0, even_in[:, :I])
+        first_pair_in = staged[:, Q * PACK :]
+        second_pair_in = sb.tile([P, 2 * I], BF16, align_bytes=MX_ALIGN)
+        turn_values(v_bf0, first_pair_in[:, :I])
+
         inv_sum = placed([P, HALVES], F32, "inv_sum", "vals0")
         nc.vector.reciprocal(inv_sum[:], row_sum[:])
         w_turned = ps.tile([P, HALVES, 2, P], F32)
         for h in range(HALVES):
             w_bf = sb.tile([P, I], BF16, name="w_bf%d" % h)
-            nc.vector.scalar_tensor_tensor(
-                w_bf[:].rearrange("q (p t) -> q p t", t=PACK), prob[h][:].rearrange("q (p t) -> q p t", t=PACK),
-                inv_sum[:, h : h + 1], size_rows[:].rearrange("q t p -> q p t"), ALU.mult, ALU.mult,
-            )
-            w_pairs = w_bf[:].bitcast(F32)
-            for u in range(2):
-                nc.tensor.transpose(w_turned[:, h, u, :], w_pairs[:, u : I // 2 : 2], ident[:])
+            nc.vector.scalar_tensor_tensor(w_bf[:], prob[h][:], inv_sum[:, h : h + 1], size_row[:], ALU.mult, ALU.mult)
+            turn_pairs(w_turned[:, h, :, :], w_bf)
         nc.scalar.copy(
             w_in.bitcast(F32).rearrange("p (h q u) -> p h q u", h=HALVES, u=2),
             w_turned[:].rearrange("p h u q -> p h q u"),
         )
         v_bf1 = sb.tile([P, I], BF16)
         nc.scalar.activation(v_bf1[:], val_pool1_bf[:].indirect(slots[:]), ACT.Copy)
-        turn_values(gather_values(2), even_in[:, I:])
+
+        turn_values(gather_values(2), first_pair_in[:, I:])
         w_codes = placed([P, Q], U32, "w_codes", "vals2")
-        w_scales = sb.tile([P, Q], U8, align_bytes=64)
+        w_scales = sb.tile([P, Q], U8, align_bytes=MX_ALIGN)
         nc.vector.quantize_mx(w_codes[:].bitcast(FP8X4), w_scales[:], w_in)
-        turn_values(v_bf1, odd_in[:, :I])
-        turn_values(gather_values(3), odd_in[:, I:])
-        reads_even = quantise_pair(0, even_in, "vals3")
-        early = [gather_background(0)]
-        reads_odd = quantise_pair(1, odd_in[:], "back0")
-        reads = [reads_even, reads_odd]
+        turn_values(v_bf1, second_pair_in[:, :I])
+        turn_values(gather_values(3), second_pair_in[:, I:])
+        banks = [read_pair(0, first_pair_in, "vals3")]
+        picked = [gather_background(j) for j in range(2)]
+        banks.append(read_pair(1, second_pair_in[:], "back1"))
 
         neg_ff = sb.tile([P, TILES], F32)
         nc.gpsimd.tensor_scalar(neg_ff[:], ff_cols[:], -1.0 / J, None, ALU.mult)
         out_by_tile = out.rearrange("(p j) q -> p j q", j=TILES)
         result = sb.tile([P, TILES - 1, Q], F32)
 
-        def sum_background(name, picked, j):
-            scaled = sb.tile([P, picked.shape[1]], F32, name="scaled" + name)
+        def sum_background(name, listed, j):
+            scaled = sb.tile([P, listed.shape[1]], F32, name="scaled" + name)
             neg_mb = sb.tile([P, 1], F32, name="neg_mb" + name)
-            nc.scalar.activation(scaled[:], picked[:], ACT.Copy, scale=neg_ff[:, j : j + 1], accum_out=neg_mb[:])
+            nc.scalar.activation(scaled[:], listed[:], ACT.Copy, scale=neg_ff[:, j : j + 1], accum_out=neg_mb[:])
             return neg_mb
 
-        for j in range(TILES - 1):
-            picked = early[j] if j < 1 else gather_background(j)
-            neg_mb = sum_background(str(j), picked, j)
-            nc.scalar.activation(result[:, j, :], reads[j % 2][:, j // 2, :], ACT.Identity, bias=neg_mb[:])
-            if j > 0:
-                done = slice(0, 2) if j == 1 else slice(2, 3)
-                nc.sync.dma_start(out_by_tile[:, done, :], result[:, done, :])
-        j = TILES - 1
-        parts = []
+        def subtract_background(j):
+            neg_mb = sum_background(str(j), picked[j], j)
+            nc.scalar.activation(result[:, j, :], banks[j // 2][:, j % 2, :], ACT.Identity, bias=neg_mb[:])
+
+        subtract_background(0)
+        subtract_background(1)
+        nc.sync.dma_start(out_by_tile[:, 0:2, :], result[:, 0:2, :])
+        picked.append(gather_background(2))
+        subtract_background(2)
+        nc.sync.dma_start(out_by_tile[:, 2:3, :], result[:, 2:3, :])
+
+        last = TILES - 1
+        half_columns = J // PER_COLUMN // 2
+        half_sums = []
         for a in range(2):
-            picked = sb.tile([P, J // 2], F32, name="picked_last%d" % a)
-            nc.vector.tensor_copy(picked[:], back_pool[j][:].indirect(slots2[:, a * J // 32 : (a + 1) * J // 32]))
-            parts.append(sum_background("_last%d" % a, picked, j))
-        last = sb.tile([P, Q], F32)
-        nc.vector.tensor_scalar(last[:], reads[j % 2][:, j // 2, :], parts[0][:], parts[1][:], ALU.add, ALU.add)
-        nc.sync.dma_start(out_by_tile[:, j, :], last[:])
+            listed = sb.tile([P, J // 2], F32, name="picked_last%d" % a)
+            offsets = slots2[:, a * half_columns : (a + 1) * half_columns]
+            nc.vector.tensor_copy(listed[:], back_pool[last][:].indirect(offsets))
+            half_sums.append(sum_background("_last%d" % a, listed, last))
+        last_result = sb.tile([P, Q], F32)
+        nc.vector.tensor_scalar(
+            last_result[:], banks[last // 2][:, last % 2, :], half_sums[0][:], half_sums[1][:], ALU.add, ALU.add
+        )
+        nc.sync.dma_start(out_by_tile[:, last, :], last_result[:])

from contextlib import ExitStack

import concourse.mybir as mybir
from concourse.masks import make_identity

D, T, I, U, J, Q, E = 512, 2048, 512, 1024, 256, 256, 512
FLOPS = 2 * Q * I * D + 2 * E * Q * I

F32 = mybir.dt.float32
BF16 = mybir.dt.bfloat16
I32 = mybir.dt.int32
U32 = mybir.dt.uint32
U16 = mybir.dt.uint16
U8 = mybir.dt.uint8
FP8X4 = mybir.dt.float8_e4m3fn_x4
FP4X4 = mybir.dt.float4_e2m1fn_x4
ALU = mybir.AluOpType
ACT = mybir.ActivationFunctionType
AXIS = mybir.AxisListType

P = 128
PACK = 4
QUADRANT = 32
PER_COLUMN = 16
LINE = 4
MX_ALIGN = 64
HALVES = Q // P
TILES = E // P
FEATURE_TILE_OF_POOL = (0, 2, 1, 3)


def tile_attend_relativeread_kernel(tc, query, keys_words, keys_scales, size, vals, back, ff, offs, offs2, out):
    nc = tc.nc
    with ExitStack() as ctx:
        sb = ctx.enter_context(tc.tile_pool(name="sb", bufs=1))
        ps = ctx.enter_context(tc.psum_pool(name="ps", bufs=1))
        ps_turn = ctx.enter_context(tc.psum_pool(name="ps_turn", bufs=2))

        def placed(shape, dtype, name, place):
            return sb.tile(shape, dtype, name=name, tag=place, align_bytes=MX_ALIGN)

        slots = sb.tile([P, I // PER_COLUMN], U16)
        slots2 = sb.tile([P, J // PER_COLUMN], U16)
        key_words = sb.tile([P, T], U16)
        key_bytes = sb.tile([P, T], U8)
        q_raw = placed([P, PACK, Q], F32, "q_raw", "queries")
        size_cols = sb.tile([P, PACK], F32)
        ff_cols = sb.tile([P, TILES], F32)
        val_pool = [placed([P, T], F32, "val_pool%d" % n, "vals%d" % n) for n in range(TILES)]
        back_pool = [placed([P, U], F32, "back_pool%d" % j, "back%d" % j) for j in range(TILES)]
        ident = sb.tile([P, P], F32)

        nc.gpsimd.memset(key_bytes[:].bitcast(I32), 0)
        make_identity(nc, ident[:])
        vals_by_tile = vals.rearrange("(p j) t -> j p t", j=TILES)
        back_by_tile = back.rearrange("(p j) u -> j p u", j=TILES)
        rows = P // QUADRANT
        nc.sync.dma_start(slots[:], offs)
        nc.sync.dma_start(key_words[:].bitcast(I32), keys_words[0].bitcast(I32))
        for r in range(rows):
            nc.sync.dma_start(
                key_bytes[r:P:QUADRANT, :].bitcast(I32), keys_scales[0, r : rows * rows : rows, :].bitcast(I32)
            )
        nc.sync.dma_start(size_cols[:], size.rearrange("o (p t) -> p (o t)", t=PACK))
        nc.sync.dma_start(q_raw[:], query.rearrange("(p t) q -> p t q", t=PACK))
        for n in range(TILES):
            nc.sync.dma_start(val_pool[n][:], vals_by_tile[FEATURE_TILE_OF_POOL[n]])
        nc.sync.dma_start(slots2[:], offs2)
        nc.sync.dma_start(ff_cols[:], ff.rearrange("(p j) o -> p (j o)", j=TILES))
        for j in range(TILES):
            nc.sync.dma_start(back_pool[j][:], back_by_tile[j])

        k_words = placed([P, I], U16, "k_words", "gathered0")
        k_bytes = sb.tile([P, I], U8, align_bytes=MX_ALIGN)
        nc.vector.tensor_copy(k_words[:], key_words[:].indirect(slots[:]))
        nc.vector.tensor_copy(k_bytes[:], key_bytes[:].indirect(slots[:]))

        scores = []
        for h in range(HALVES):
            q_bf = sb.tile([P, P, PACK], BF16, name="q_bf%d" % h, align_bytes=MX_ALIGN)
            q_codes = sb.tile([P, P], U32, name="q_codes%d" % h, align_bytes=MX_ALIGN)
            q_scales = sb.tile([P, P], U8, name="q_scales%d" % h, align_bytes=MX_ALIGN)
            nc.scalar.copy(
                q_bf[:].rearrange("p (c i) t -> p c t i", i=LINE),
                q_raw[:, :, h * P : (h + 1) * P].rearrange("p t (c i) -> p c t i", i=LINE),
            )
            nc.vector.quantize_mx(q_codes[:].bitcast(FP8X4), q_scales[:], q_bf[:].rearrange("p q t -> p (q t)"))
            scores.append(ps.tile([P, I], F32, name="scores%d" % h))
            nc.tensor.matmul_mx(
                out=scores[h][:], lhsT=q_codes[:].bitcast(FP8X4), lhsT_scale=q_scales[:],
                rhs=k_words[:].bitcast(FP4X4), rhs_scale=k_bytes[:], start=True, stop=True,
            )

        size_turned = ps.tile([P, PACK, P], F32)
        for t in range(PACK):
            nc.tensor.transpose(size_turned[:, t, :], size_cols[:, t : t + 1].to_broadcast([P, P]), ident[:])
        size_row = placed([P, I], F32, "size_row", "queries")
        nc.scalar.copy(size_row[:].rearrange("q (p t) -> q p t", t=PACK), size_turned[:].rearrange("q t p -> q p t"))

        def gather_values(n):
            v_bf = placed([P, I], BF16, "v_bf%d" % n, "gathered%d" % n)
            nc.vector.tensor_copy(v_bf[:], val_pool[n][:].indirect(slots[:]))
            return v_bf

        def turn_pairs(turned, by_slot):
            pairs = by_slot[:].bitcast(F32)
            for u in range(2):
                nc.tensor.transpose(turned[:, u, :], pairs[:, u : I // 2 : 2], ident[:])

        def turn_values(v_bf, v_in):
            v_turned = ps_turn.tile([P, 2, P], F32)
            turn_pairs(v_turned[:], v_bf)
            nc.scalar.copy(v_in.bitcast(F32).rearrange("p (e u) -> p e u", u=2), v_turned[:].rearrange("p u e -> p e u"))

        def gather_background(j):
            picked = sb.tile([P, J], F32, name="picked%d" % j)
            nc.vector.tensor_copy(picked[:], back_pool[j][:].indirect(slots2[:]))
            return picked

        def read_pair(b, v_in, place):
            v_codes = placed([P, 2 * P], U32, "v_codes%d" % b, place)
            v_scales = sb.tile([P, 2 * P], U8, name="v_scales%d" % b, align_bytes=MX_ALIGN)
            nc.vector.quantize_mx(v_codes[:].bitcast(FP8X4), v_scales[:], v_in)
            bank = ps.tile([P, 2, Q], F32, name="reads%d" % b)
            for a in range(2):
                cols = slice(a * P, (a + 1) * P)
                nc.tensor.matmul_mx(
                    out=bank[:, a, :], lhsT=v_codes[:, cols].bitcast(FP8X4), lhsT_scale=v_scales[:, cols],
                    rhs=w_codes[:].bitcast(FP8X4), rhs_scale=w_scales[:], start=True, stop=True,
                )
            return bank

        row_sum = sb.tile([P, HALVES], F32)
        prob = []
        for h in range(HALVES):
            neg_max = sb.tile([P, 1], F32, name="neg_max%d" % h)
            prob.append(sb.tile([P, I], F32, name="prob%d" % h))
            nc.vector.tensor_reduce(neg_max[:], scores[h][:], AXIS.X, ALU.max, negate=True)
            nc.scalar.activation(prob[h][:], scores[h][:], ACT.Exp, bias=neg_max[:], accum_out=row_sum[:, h : h + 1])

        v_bf0 = gather_values(0)
        val_pool1_bf = sb.tile([P, T], BF16)
        nc.scalar.activation(val_pool1_bf[:], val_pool[1][:], ACT.Copy)
        staged = placed([P, Q * PACK + 2 * I], BF16, "staged", "vals1")
        w_in = staged[:, : Q * PACK]
        first_pair_in = staged[:, Q * PACK :]
        second_pair_in = sb.tile([P, 2 * I], BF16, align_bytes=MX_ALIGN)
        turn_values(v_bf0, first_pair_in[:, :I])

        inv_sum = placed([P, HALVES], F32, "inv_sum", "vals0")
        nc.vector.reciprocal(inv_sum[:], row_sum[:])
        w_turned = ps.tile([P, HALVES, 2, P], F32)
        for h in range(HALVES):
            w_bf = sb.tile([P, I], BF16, name="w_bf%d" % h)
            nc.vector.scalar_tensor_tensor(w_bf[:], prob[h][:], inv_sum[:, h : h + 1], size_row[:], ALU.mult, ALU.mult)
            turn_pairs(w_turned[:, h, :, :], w_bf)
        nc.scalar.copy(
            w_in.bitcast(F32).rearrange("p (h q u) -> p h q u", h=HALVES, u=2),
            w_turned[:].rearrange("p h u q -> p h q u"),
        )
        v_bf1 = sb.tile([P, I], BF16)
        nc.scalar.activation(v_bf1[:], val_pool1_bf[:].indirect(slots[:]), ACT.Copy)

        turn_values(gather_values(2), first_pair_in[:, I:])
        w_codes = placed([P, Q], U32, "w_codes", "vals2")
        w_scales = sb.tile([P, Q], U8, align_bytes=MX_ALIGN)
        nc.vector.quantize_mx(w_codes[:].bitcast(FP8X4), w_scales[:], w_in)
        turn_values(v_bf1, second_pair_in[:, :I])
        turn_values(gather_values(3), second_pair_in[:, I:])
        banks = [read_pair(0, first_pair_in, "vals3")]
        picked = [gather_background(j) for j in range(2)]
        banks.append(read_pair(1, second_pair_in[:], "back1"))

        neg_ff = sb.tile([P, TILES], F32)
        nc.gpsimd.tensor_scalar(neg_ff[:], ff_cols[:], -1.0 / J, None, ALU.mult)
        out_by_tile = out.rearrange("(p j) q -> p j q", j=TILES)
        result = sb.tile([P, TILES - 1, Q], F32)

        def sum_background(name, listed, j):
            scaled = sb.tile([P, listed.shape[1]], F32, name="scaled" + name)
            neg_mb = sb.tile([P, 1], F32, name="neg_mb" + name)
            nc.scalar.activation(scaled[:], listed[:], ACT.Copy, scale=neg_ff[:, j : j + 1], accum_out=neg_mb[:])
            return neg_mb

        def subtract_background(j):
            neg_mb = sum_background(str(j), picked[j], j)
            nc.scalar.activation(result[:, j, :], banks[j // 2][:, j % 2, :], ACT.Identity, bias=neg_mb[:])

        subtract_background(0)
        subtract_background(1)
        nc.sync.dma_start(out_by_tile[:, 0:2, :], result[:, 0:2, :])
        picked.append(gather_background(2))
        subtract_background(2)
        nc.sync.dma_start(out_by_tile[:, 2:3, :], result[:, 2:3, :])

        last = TILES - 1
        half_columns = J // PER_COLUMN // 2
        half_sums = []
        for a in range(2):
            listed = sb.tile([P, J // 2], F32, name="picked_last%d" % a)
            offsets = slots2[:, a * half_columns : (a + 1) * half_columns]
            nc.vector.tensor_copy(listed[:], back_pool[last][:].indirect(offsets))
            half_sums.append(sum_background("_last%d" % a, listed, last))
        last_result = sb.tile([P, Q], F32)
        nc.vector.tensor_scalar(
            last_result[:], banks[last // 2][:, last % 2, :], half_sums[0][:], half_sums[1][:], ALU.add, ALU.add
        )
        nc.sync.dma_start(out_by_tile[:, last, :], last_result[:])
